import numpy as np
import ml_dtypes


def mxq(x, axis, fmt="e4m3"):
    dtype, down = {"e4m3": (ml_dtypes.float8_e4m3fn, 7), "e5m2": (ml_dtypes.float8_e5m2, 14)}[fmt]
    v = np.moveaxis(np.asarray(x, np.float32).astype(ml_dtypes.bfloat16).astype(np.float64), axis, -1)
    blocks = v.reshape(v.shape[:-1] + (-1, 32))
    amax = np.abs(blocks).max(-1, keepdims=True)
    byte = np.maximum(np.where(amax > 0, np.frexp(amax)[1] - 1 + 127, 0) - down, 1)
    scale = np.exp2(byte - 127.0)
    codes = (blocks / scale).astype(np.float32).astype(dtype).astype(np.float64)
    return np.moveaxis((codes * scale).reshape(v.shape), -1, axis)


WIDE = False


def mx_kscale(k):
    if not WIDE:
        return np.ones(k)
    levels = np.array([10, -10, 5, -5, 0])
    if k % 512:
        return np.exp2(np.random.permutation(np.resize(levels, k // 32))).repeat(32)
    a = np.empty((k // 512, 16))
    for p in range(k // 512):
        a[p, :8] = np.random.permutation(np.resize(levels, 8))
        for g in range(8):
            far = levels[np.abs(levels - a[p, g]) >= 10]
            a[p, g + 8] = far[np.random.randint(len(far))]
    return np.exp2(a.ravel()).repeat(32)


def f64(x):
    return np.asarray(x).astype(np.float64)


def striped(idx):
    return np.tile(idx.reshape(-1, 16).T, (8, 1)).astype(np.uint16)


def unstriped(offs):
    return offs[:16].T.reshape(-1).astype(np.int64)


def striped8(idx):
    return np.concatenate([x.reshape(-1, 16).T for x in idx]).astype(np.uint16)


def runs(offs, k):
    lists = np.stack([offs[16 * r : 16 * r + 16].T.reshape(-1) for r in range(8)]).astype(np.int64)
    return lists[np.arange(k) % 512 // 64]


def pack_weight(w):
    k, n = w.shape
    w = f64(np.asarray(w, np.float32).astype(ml_dtypes.bfloat16)).reshape(k // 32, 32, n)
    amax = np.abs(w).max(1)
    byte = np.clip(np.where(amax > 0, np.frexp(amax)[1] - 1 + 127 - 7, 1), 1, 254)
    scaled = (w * np.exp2(127.0 - byte)[:, None, :]).reshape(k, n).astype(np.float32)
    words = np.ascontiguousarray(scaled.reshape(k // 512, 128, 4, n).transpose(0, 1, 3, 2)).astype(ml_dtypes.float8_e4m3fn).view(np.uint8)
    return words, np.ascontiguousarray(byte.astype(np.uint8).reshape(k // 512, 16, n))


def unpack_weight(words, scales):
    g, p, n, _ = words.shape
    vals = np.ascontiguousarray(words).view(ml_dtypes.float8_e4m3fn).astype(np.float64) * np.repeat(np.exp2(scales.astype(np.float64) - 127.0), 8, axis=1)[..., None]
    return vals.transpose(0, 1, 3, 2).reshape(g * 512, n)


def sigmoid(v):
    return 1.0 / (1.0 + np.exp(-np.maximum(v, -700.0)))

def planes(y):
    n, m = y.shape
    v = y.astype(np.float32).astype(ml_dtypes.bfloat16).astype(np.float64).reshape(n // 32, 32, m)
    top = np.abs(v).max(1)
    byte = np.clip(np.where(top > 0, np.frexp(top)[1] - 1 + 127 - 7, 1), 1, 254)
    codes = (v * np.exp2(127.0 - byte)[:, None, :]).reshape(n, m).astype(np.float32).astype(ml_dtypes.float8_e4m3fn).view(np.uint8)
    words = codes.reshape(n // 512, 128, 4, m).transpose(0, 1, 3, 2)
    return np.ascontiguousarray(words), np.ascontiguousarray(byte.astype(np.uint8).reshape(n // 512, 16, m))


K, T, S, N, H, U = 512, 2048, 512, 512, 512, 1024


def setup_inputs():
    n = np.random.standard_normal
    s = mx_kscale(K)[:, None]
    u = mx_kscale(H)
    packed_xT = pack_weight(n((K, T)) * s)
    packed_w1 = pack_weight(n((K, H)) / np.sqrt(K) / s)
    packed_w2 = pack_weight(n((K, H)) / np.sqrt(K) / s)
    packed_w3 = pack_weight(n((H, N)) / np.sqrt(H) / u[:, None])
    return {
        "x_words": packed_xT[0],
        "x_scales": packed_xT[1],
        "w1_words": packed_w1[0],
        "w1_scales": packed_w1[1],
        "w2_words": packed_w2[0],
        "w2_scales": packed_w2[1],
        "gn": (np.random.uniform(0.5, 1.5, (H, 1)) * u[:, None]).astype(np.float32),
        "w3_words": packed_w3[0],
        "w3_scales": packed_w3[1],
        "mem": n((N, U)).astype(np.float32),
        "offs": striped(np.random.permutation(T)[:S]),
        "hz": striped8(np.random.randint(0, T, (8, S))),
        "n1": striped(np.random.permutation(S)),
        "n2": striped(np.random.permutation(S)),
        "n3": striped8(np.stack([np.random.permutation(U)[:S] for _ in range(8)])),
        "n4": striped8(np.stack([np.random.permutation(U) for _ in range(8)])),
    }


def reference(x_words, x_scales, w1_words, w1_scales, w2_words, w2_scales, gn, w3_words, w3_scales, mem, offs, hz, n1, n2, n3, n4):
    xq = unpack_weight(x_words, x_scales)[:, unstriped(offs)]
    y = unpack_weight(w1_words, w1_scales).T @ xq
    x_hz = unpack_weight(x_words, x_scales)[np.arange(K)[:, None], runs(hz, K)]
    d = unpack_weight(w2_words, w2_scales).T @ x_hz
    z = f64(gn) * (y + (sigmoid(d[:, unstriped(n2)] - d)) * (y[:, unstriped(n1)] - y))
    h = unpack_weight(w3_words, w3_scales).T @ mxq(z, 0, "e4m3")
    pg = f64(mem).copy()
    pg[np.arange(N)[:, None], runs(n3, N)] = h
    out_0 = pg - (0.5 * (pg[np.arange(N)[:, None], runs(n4, N)]))
    return (out_0,) + planes(out_0)

@@ -1,0 +1,238 @@
+from contextlib import ExitStack
+
+import concourse.mybir as mybir
+
+F32 = mybir.dt.float32
+BF16 = mybir.dt.bfloat16
+I32 = mybir.dt.int32
+U32 = mybir.dt.uint32
+U16 = mybir.dt.uint16
+U8 = mybir.dt.uint8
+FP8X4 = mybir.dt.float8_e4m3fn_x4
+ACT = mybir.ActivationFunctionType
+ALU = mybir.AluOpType
+
+P = 128
+PACK = 4
+T, S, U = 2048, 512, 1024
+HALF = S // 2
+FLOPS = 3 * 2 * 512 * 512 * 512
+
+
+def tile_picked_twhpullbpagem_none_po_kernel(
+    tc, x_words, x_scales, w1_words, w1_scales, w2_words, w2_scales, gn, w3_words, w3_scales,
+    mem, offs, hz, n1, n2, n3, n4, out_0, out_1, out_2,
+):
+    nc = tc.nc
+    with ExitStack() as ctx:
+        keep = ctx.enter_context(tc.tile_pool(name="keep", bufs=1))
+        early = ctx.enter_context(tc.tile_pool(name="early", bufs=1))
+        psum = ctx.enter_context(tc.psum_pool(name="psum", bufs=1))
+
+        def tile(shape, dtype, name):
+            return keep.tile(shape, dtype, name=name, align_bytes=64)
+
+        def load_list(src, name):
+            dst = tile(list(src.shape), U16, name)
+            nc.sync.dma_start(dst[:], src)
+            return dst
+
+        def words_view(src):
+            return src[0].rearrange("p n t -> p (n t)").bitcast(I32)
+
+        def entries(lst, start, count):
+            return lst[:, start // 16 : (start + count) // 16]
+
+        def load_scale_rows(queue, dst, first, src):
+            for q in range(4):
+                queue.dma_start(dst[32 * q + first : 32 * q + first + 4, :].bitcast(I32), src[0, 4 * q : 4 * q + 4, :].bitcast(I32))
+
+        def deal_words(raw, name):
+            dealt = tile([P, S], U32, name)
+            nc.scalar.copy(dealt[:].rearrange("p (t m) -> p m t", t=PACK), raw[:].bitcast(U32).rearrange("p (m t) -> p m t", t=PACK))
+            return dealt
+
+        def deal_scales(raw, name):
+            dealt = tile([P, S], U8, name)
+            nc.vector.tensor_copy(dealt[:].rearrange("p (t m) -> p m t", t=PACK), raw[:].rearrange("p (m t) -> p m t", t=PACK))
+            return dealt
+
+        xs = early.tile([P, T], U8, name="xs", offset=3 * 4 * U - T // 2)
+        nc.gpsimd.memset(xs[:].bitcast(I32), 0)
+        w2s_raw = tile([P, S], U8, "w2s_raw")
+        w13s_raw = tile([P, S], U8, "w13s_raw")
+        nc.gpsimd.memset(w2s_raw[:].bitcast(I32), 0)
+        nc.gpsimd.memset(w13s_raw[:].bitcast(I32), 0)
+
+        hz_sb = load_list(hz, "hz_sb")
+        offs_sb = load_list(offs, "offs_sb")
+        xs32, xsrc32 = xs[:].bitcast(I32), x_scales[0].bitcast(I32)
+        for e in range(2):
+            nc.sync.dma_start(xs32[e:P:16, :], xsrc32[e:16:2, :])
+        for r in (2, 3):
+            nc.sync.dma_start(xs32[r:P:32, :], xsrc32[r:16:4, :])
+        xw = early.tile([P, T], I32, name="xw", offset=0)
+        nc.sync.dma_start(xw[:], words_view(x_words))
+        ww_raw = [tile([P, S], I32, f"ww_raw{i}") for i in range(2)]
+        nc.sync.dma_start(ww_raw[1][:], words_view(w2_words))
+        load_scale_rows(nc.sync, w2s_raw, 0, w2_scales)
+
+        xh_s_raw = tile([P, S], U8, "xh_s_raw")
+        nc.vector.tensor_copy(xh_s_raw[:], xs[:].indirect(hz_sb[:]))
+        xh_s = tile([P, S], U8, "xh_s")
+        nc.vector.tensor_copy(xh_s[:].bitcast(I32), xh_s_raw[:].bitcast(I32))
+        for e in range(2):
+            nc.sync.dma_start(xh_s[:].bitcast(I32)[2 + e : P : 32, :], xh_s_raw[:].bitcast(I32)[16 + e : P : 32, :])
+        xq_s = tile([P, S], U8, "xq_s")
+        nc.vector.tensor_copy(xq_s[:], xs[:].indirect(offs_sb[:]))
+        w2_s = deal_scales(w2s_raw, "w2_s")
+        xh_w = tile([P, S], U32, "xh_w")
+        nc.vector.tensor_copy(xh_w[:], xw[:].bitcast(U32).indirect(hz_sb[:]))
+        xq_w = tile([P, S], U32, "xq_w")
+        nc.vector.tensor_copy(xq_w[:], xw[:].bitcast(U32).indirect(offs_sb[:]))
+
+        nc.sync.dma_start(ww_raw[0][:], words_view(w1_words))
+        load_scale_rows(nc.sync, w13s_raw, 0, w1_scales)
+        n2_sb = load_list(n2, "n2_sb")
+        n1_sb = load_list(n1, "n1_sb")
+        gain = tile([P, PACK], F32, "gain")
+        nc.sync.dma_start(gain[:], gn.rearrange("(p t) o -> p (t o)", t=PACK))
+        n3_sb = load_list(n3, "n3_sb")
+        page = [early.tile([P, U], F32, name=f"page{t}", offset=4 * U * t) for t in range(PACK)]
+        mem_rows = mem.rearrange("(p t) w -> t p w", t=PACK)
+        n4_sb = load_list(n4, "n4_sb")
+
+        w2_w = deal_words(ww_raw[1], "w2_w")
+        w1_w = deal_words(ww_raw[0], "w1_w")
+        w1_s = deal_scales(w13s_raw, "w13_s")
+        load_scale_rows(nc.sync, w2s_raw, 0, w3_scales)
+        nc.sync.dma_start(ww_raw[1][:], words_view(w3_words))
+        for t in (2, 3, 0, 1):
+            nc.sync.dma_start(page[t][:], mem_rows[t])
+
+        def product(acc, w_w, w_s, t, a_w, a_s):
+            cols = slice(t * P, (t + 1) * P)
+            nc.tensor.matmul_mx(out=acc, lhsT=w_w[:, cols].bitcast(FP8X4), lhsT_scale=w_s[:, cols],
+                                rhs=a_w.bitcast(FP8X4), rhs_scale=a_s, start=True, stop=True)
+
+        d_ps = [psum.tile([P, S], F32, name=f"d_ps{t}") for t in range(PACK)]
+        d_sb = [tile([P, S], F32, f"d_sb{t}") for t in range(PACK)]
+        y_sb = [tile([P, S], F32, f"y_sb{t}") for t in range(PACK)]
+        y_ps = [psum.tile([P, S], F32, name=f"y_ps{t}", tag=f"bank{t}") for t in range(PACK)]
+        for t in range(PACK):
+            product(d_ps[t][:], w2_w, w2_s, t, xh_w[:], xh_s[:])
+        for t in range(PACK):
+            product(y_ps[t][:], w1_w, w1_s, t, xq_w[:], xq_s[:])
+
+        pulled = tile([P, PACK, S], F32, "pulled")
+        held = tile([P, PACK, S], F32, "held")
+        gate = [tile([P, S], F32, f"gate{t}") for t in range(PACK)]
+        diff = [tile([P, S], F32, f"diff{t}") for t in range(PACK)]
+
+        def front(t):
+            nc.scalar.copy(d_sb[t][:], d_ps[t][:])
+            far = tile([P, S], F32, f"far{t}")
+            for c0 in (0, HALF):
+                nc.scalar.activation(far[:, c0 : c0 + HALF], d_sb[t][:].indirect(entries(n2_sb, c0, HALF)), ACT.Copy)
+            if t < 2:
+                nc.vector.tensor_scalar(y_sb[t][:], y_ps[t][:], gain[:, t : t + 1], None, ALU.mult)
+            nc.vector.tensor_tensor(diff[t][:], far[:], d_ps[t][:], ALU.subtract)
+
+        def back(t):
+            nc.scalar.activation(gate[t][:], diff[t][:], ACT.Sigmoid)
+            if t in (1, 2):
+                nc.scalar.activation(y_sb[t + 1][:], y_ps[t + 1][:], ACT.Copy, scale=gain[:, t + 1 : t + 2])
+            if t < PACK - 1:
+                for c0 in (0, HALF):
+                    nc.vector.tensor_tensor(pulled[:, t, c0 : c0 + HALF], y_sb[t][:].indirect(entries(n1_sb, c0, HALF)), gate[t][:, c0 : c0 + HALF], ALU.mult)
+            nc.vector.scalar_tensor_tensor(held[:, t, :], gate[t][:], 1.0, y_sb[t][:], ALU.subtract, ALU.mult)
+            if t == PACK - 1:
+                near = tile([P, S], F32, "near")
+                for c0 in (0, HALF):
+                    nc.scalar.activation(near[:, c0 : c0 + HALF], y_sb[t][:].indirect(entries(n1_sb, c0, HALF)), ACT.Copy)
+                nc.vector.tensor_tensor(pulled[:, t, :], near[:], gate[t][:], ALU.mult)
+
+        front(0)
+        for t in range(PACK):
+            if t + 1 < PACK:
+                front(t + 1)
+            if t == 1:
+                w3_s = deal_scales(w2s_raw, "w3_s")
+            if t == 3:
+                w3_w = deal_words(ww_raw[1], "w3_w")
+            back(t)
+
+        z_bf = [tile([P, HALF * PACK], BF16, f"z_bf{half}") for half in range(2)]
+        z_w = [tile([P, HALF], U32, f"z_w{half}") for half in range(2)]
+        z_s = [tile([P, HALF], U8, f"z_s{half}") for half in range(2)]
+        h_sb = tile([P, PACK, S], F32, "h_sb")
+        for half in range(2):
+            cols = slice(half * HALF, (half + 1) * HALF)
+            nc.vector.tensor_tensor(
+                z_bf[half][:].rearrange("p (c i t) -> p c t i", i=4, t=PACK),
+                pulled[:, :, cols].rearrange("p t (c i) -> p c t i", i=4),
+                held[:, :, cols].rearrange("p t (c i) -> p c t i", i=4),
+                ALU.subtract,
+            )
+            nc.vector.quantize_mx(out=z_w[half][:].bitcast(FP8X4), scales=z_s[half][:], in_=z_bf[half][:])
+            for pair in range(2):
+                h_ps = psum.tile([P, 2, HALF], F32, name=f"h_ps{half}_{pair}", tag=f"bank{2 * half + pair}")
+                for e in range(2):
+                    product(h_ps[:, e, :], w3_w, w3_s, 2 * pair + e, z_w[half][:], z_s[half][:])
+                nc.scalar.copy(h_sb[:, 2 * pair : 2 * pair + 2, cols], h_ps[:])
+
+        result = tile([P, PACK, U], F32, "result")
+        out_rows = out_0.rearrange("(p t) w -> t p w", t=PACK)
+        CH = 512
+
+        def scatter(t):
+            width = HALF if t == 0 else S
+            for c0 in range(0, S, width):
+                nc.vector.tensor_copy(page[t][:].indirect(entries(n3_sb, c0, width)), h_sb[:, t, c0 : c0 + width])
+
+        def finish(t):
+            for c0 in range(0, U, CH):
+                other = tile([P, CH], F32, f"other{t}_{c0}")
+                nc.scalar.activation(other[:], page[t][:].indirect(entries(n4_sb, c0, CH)), ACT.Copy, scale=-0.5)
+                adder = nc.gpsimd if t < PACK - 1 else nc.vector
+                adder.tensor_tensor(result[:, t, c0 : c0 + CH], other[:], page[t][:, c0 : c0 + CH], ALU.add)
+                nc.sync.dma_start(out_rows[t][:, c0 : c0 + CH], result[:, t, c0 : c0 + CH])
+
+        for t in range(PACK):
+            scatter(t)
+        for t in range(PACK - 1):
+            finish(t)
+
+        o_w = tile([P, U], U32, "o_w")
+        o_s = tile([P, U], U8, "o_s")
+        QC = 256
+        out_words = words_view(out_1)
+        last = PACK - 1
+        order = (3, 0, 1, 2)
+        for k in order:
+            c0 = k * QC
+            other = tile([P, QC], F32, f"other{last}_{c0}")
+            looked = page[last][:].indirect(entries(n4_sb, c0, QC))
+            if k == 3:
+                nc.vector.tensor_copy(other[:], looked)
+            else:
+                nc.scalar.activation(other[:], looked, ACT.Copy)
+            nc.vector.scalar_tensor_tensor(result[:, last, c0 : c0 + QC], other[:], -0.5, page[last][:, c0 : c0 + QC], ALU.mult, ALU.add)
+        for c0 in (CH, 0):
+            nc.sync.dma_start(out_rows[last][:, c0 : c0 + CH], result[:, last, c0 : c0 + CH])
+        o_bf = {}
+        for n, k in enumerate(order):
+            c0 = k * QC
+            o_bf[k] = tile([P, QC * PACK], BF16, f"o_bf{k}")
+            dst = o_bf[k][:].rearrange("p (c i t) -> p c t i", i=4, t=PACK)
+            src = result[:, :, c0 : c0 + QC].rearrange("p t (c i) -> p c t i", i=4)
+            if n % 2 == 0:
+                nc.vector.tensor_copy(dst, src)
+            else:
+                nc.scalar.copy(dst, src)
+        for k in (3, 1, 0, 2):
+            c0 = k * QC
+            nc.vector.quantize_mx(out=o_w[:, c0 : c0 + QC].bitcast(FP8X4), scales=o_s[:, c0 : c0 + QC], in_=o_bf[k][:])
+            nc.sync.dma_start(out_words[:, c0 : c0 + QC], o_w[:, c0 : c0 + QC].bitcast(I32))
+        for q in range(4):
+            nc.sync.dma_start(out_2[0, 4 * q : 4 * q + 4, :].bitcast(I32), o_s[32 * q : 32 * q + 4, :].bitcast(I32))

@@ -14,8 +14,16 @@ ALU = mybir.AluOpType
 
 P = 128
 PACK = 4
+LAST = PACK - 1
+QUADRANT = 32
+GROUP = 16
 T, S, U = 2048, 512, 1024
 HALF = S // 2
+PAGE_HALF = U // 2
+CHUNK = U // 4
+LINE = 4
+PAGE_BYTES = 4 * U
+ROW_BYTES = 4 * S
 FLOPS = 3 * 2 * 512 * 512 * 512
 
 
@@ -26,11 +34,11 @@ def tile_picked_twhpullbpagem_none_po_kernel(
     nc = tc.nc
     with ExitStack() as ctx:
         keep = ctx.enter_context(tc.tile_pool(name="keep", bufs=1))
-        early = ctx.enter_context(tc.tile_pool(name="early", bufs=1))
+        reused = ctx.enter_context(tc.tile_pool(name="reused", bufs=1))
         psum = ctx.enter_context(tc.psum_pool(name="psum", bufs=1))
 
-        def tile(shape, dtype, name):
-            return keep.tile(shape, dtype, name=name, align_bytes=64)
+        def tile(shape, dtype, name, after=""):
+            return keep.tile(shape, dtype, name=name, tag=after or name, align_bytes=64)
 
         def load_list(src, name):
             dst = tile(list(src.shape), U16, name)
@@ -41,139 +49,169 @@ def tile_picked_twhpullbpagem_none_po_kernel(
             return src[0].rearrange("p n t -> p (n t)").bitcast(I32)
 
         def entries(lst, start, count):
-            return lst[:, start // 16 : (start + count) // 16]
+            return lst[:, start // GROUP : (start + count) // GROUP]
 
-        def load_scale_rows(queue, dst, first, src):
-            for q in range(4):
-                queue.dma_start(dst[32 * q + first : 32 * q + first + 4, :].bitcast(I32), src[0, 4 * q : 4 * q + 4, :].bitcast(I32))
+        def load_scale_rows(dst, src):
+            for q in range(P // QUADRANT):
+                nc.sync.dma_start(
+                    dst[QUADRANT * q : QUADRANT * q + 4, :].bitcast(I32), src[0, 4 * q : 4 * q + 4, :].bitcast(I32)
+                )
 
-        def deal_words(raw, name):
-            dealt = tile([P, S], U32, name)
-            nc.scalar.copy(dealt[:].rearrange("p (t m) -> p m t", t=PACK), raw[:].bitcast(U32).rearrange("p (m t) -> p m t", t=PACK))
+        def deal_words(raw, name, after=""):
+            dealt = tile([P, S], U32, name, after)
+            nc.scalar.copy(
+                dealt[:].rearrange("p (t m) -> p m t", t=PACK), raw[:].bitcast(U32).rearrange("p (m t) -> p m t", t=PACK)
+            )
             return dealt
 
-        def deal_scales(raw, name):
-            dealt = tile([P, S], U8, name)
-            nc.vector.tensor_copy(dealt[:].rearrange("p (t m) -> p m t", t=PACK), raw[:].rearrange("p (m t) -> p m t", t=PACK))
+        def deal_scales(raw, name, after=""):
+            dealt = tile([P, S], U8, name, after)
+            nc.vector.tensor_copy(
+                dealt[:].rearrange("p (t m) -> p m t", t=PACK), raw[:].rearrange("p (m t) -> p m t", t=PACK)
+            )
             return dealt
 
-        xs = early.tile([P, T], U8, name="xs", offset=3 * 4 * U - T // 2)
-        nc.gpsimd.memset(xs[:].bitcast(I32), 0)
-        w2s_raw = tile([P, S], U8, "w2s_raw")
-        w13s_raw = tile([P, S], U8, "w13s_raw")
-        nc.gpsimd.memset(w2s_raw[:].bitcast(I32), 0)
-        nc.gpsimd.memset(w13s_raw[:].bitcast(I32), 0)
+        def woven(dst):
+            return dst.rearrange("p (c i t) -> p c t i", i=LINE, t=PACK)
 
-        hz_sb = load_list(hz, "hz_sb")
-        offs_sb = load_list(offs, "offs_sb")
-        xs32, xsrc32 = xs[:].bitcast(I32), x_scales[0].bitcast(I32)
-        for e in range(2):
-            nc.sync.dma_start(xs32[e:P:16, :], xsrc32[e:16:2, :])
-        for r in (2, 3):
-            nc.sync.dma_start(xs32[r:P:32, :], xsrc32[r:16:4, :])
-        xw = early.tile([P, T], I32, name="xw", offset=0)
-        nc.sync.dma_start(xw[:], words_view(x_words))
-        ww_raw = [tile([P, S], I32, f"ww_raw{i}") for i in range(2)]
-        nc.sync.dma_start(ww_raw[1][:], words_view(w2_words))
-        load_scale_rows(nc.sync, w2s_raw, 0, w2_scales)
+        def by_lines(src):
+            return src.rearrange("p t (c i) -> p c t i", i=LINE)
 
-        xh_s_raw = tile([P, S], U8, "xh_s_raw")
-        nc.vector.tensor_copy(xh_s_raw[:], xs[:].indirect(hz_sb[:]))
-        xh_s = tile([P, S], U8, "xh_s")
-        nc.vector.tensor_copy(xh_s[:].bitcast(I32), xh_s_raw[:].bitcast(I32))
-        for e in range(2):
-            nc.sync.dma_start(xh_s[:].bitcast(I32)[2 + e : P : 32, :], xh_s_raw[:].bitcast(I32)[16 + e : P : 32, :])
-        xq_s = tile([P, S], U8, "xq_s")
-        nc.vector.tensor_copy(xq_s[:], xs[:].indirect(offs_sb[:]))
-        w2_s = deal_scales(w2s_raw, "w2_s")
-        xh_w = tile([P, S], U32, "xh_w")
-        nc.vector.tensor_copy(xh_w[:], xw[:].bitcast(U32).indirect(hz_sb[:]))
-        xq_w = tile([P, S], U32, "xq_w")
-        nc.vector.tensor_copy(xq_w[:], xw[:].bitcast(U32).indirect(offs_sb[:]))
-
-        nc.sync.dma_start(ww_raw[0][:], words_view(w1_words))
-        load_scale_rows(nc.sync, w13s_raw, 0, w1_scales)
-        n2_sb = load_list(n2, "n2_sb")
-        n1_sb = load_list(n1, "n1_sb")
+        x_scale_rows = tile([P, T], U8, "x_scale_rows")
+        nc.gpsimd.memset(x_scale_rows[:].bitcast(I32), 0)
+        w1_scale_rows = reused.tile([P, S], U8, name="w1_scale_rows", offset=2 * PAGE_BYTES, align_bytes=64)
+        w2_scale_rows = reused.tile(
+            [P, S], U8, name="w2_scale_rows", offset=PACK * PAGE_BYTES + ROW_BYTES - S // 2, align_bytes=64
+        )
+        nc.gpsimd.memset(w1_scale_rows[:].bitcast(I32), 0)
+        nc.gpsimd.memset(w2_scale_rows[:].bitcast(I32), 0)
         gain = tile([P, PACK], F32, "gain")
-        nc.sync.dma_start(gain[:], gn.rearrange("(p t) o -> p (t o)", t=PACK))
-        n3_sb = load_list(n3, "n3_sb")
-        page = [early.tile([P, U], F32, name=f"page{t}", offset=4 * U * t) for t in range(PACK)]
-        mem_rows = mem.rearrange("(p t) w -> t p w", t=PACK)
-        n4_sb = load_list(n4, "n4_sb")
+        nc.gpsimd.dma_start(gain[:], gn.rearrange("(p t) o -> p (t o)", t=PACK))
+        hz_list = load_list(hz, "hz_list")
+        offs_list = load_list(offs, "offs_list")
+        rows_dst, rows_src = x_scale_rows[:].bitcast(I32), x_scales[0].bitcast(I32)
+        for e in range(2):
+            nc.sync.dma_start(rows_dst[e:P:GROUP, :], rows_src[e:16:2, :])
+        for r in (2, 3):
+            nc.sync.dma_start(rows_dst[r:P:QUADRANT, :], rows_src[r:16:4, :])
+        x_table = reused.tile([P, T], I32, name="x_table", offset=0)
+        nc.sync.dma_start(x_table[:], words_view(x_words))
+        w1_raw = tile([P, S], I32, "w1_raw")
+        w23_raw = tile([P, S], I32, "w23_raw")
+        nc.sync.dma_start(w1_raw[:], words_view(w1_words))
+        load_scale_rows(w1_scale_rows, w1_scales)
+        nc.sync.dma_start(w23_raw[:], words_view(w2_words))
+        n1_list = load_list(n1, "n1_list")
 
-        w2_w = deal_words(ww_raw[1], "w2_w")
-        w1_w = deal_words(ww_raw[0], "w1_w")
-        w1_s = deal_scales(w13s_raw, "w13_s")
-        load_scale_rows(nc.sync, w2s_raw, 0, w3_scales)
-        nc.sync.dma_start(ww_raw[1][:], words_view(w3_words))
-        for t in (2, 3, 0, 1):
+        hashed_rows = tile([P, S], U8, "hashed_rows")
+        nc.vector.tensor_copy(hashed_rows[:], x_scale_rows[:].indirect(hz_list[:]))
+        hashed_s = tile([P, S], U8, "hashed_s")
+        nc.vector.tensor_copy(hashed_s[:].bitcast(I32), hashed_rows[:].bitcast(I32))
+        for e in range(2):
+            nc.sync.dma_start(
+                hashed_s[:].bitcast(I32)[2 + e : P : QUADRANT, :], hashed_rows[:].bitcast(I32)[GROUP + e : P : QUADRANT, :]
+            )
+        load_scale_rows(w2_scale_rows, w2_scales)
+        n2_list = load_list(n2, "n2_list")
+        n3_list = load_list(n3, "n3_list")
+        n4_list = load_list(n4, "n4_list")
+        picked_s = tile([P, S], U8, "picked_s")
+        nc.vector.tensor_copy(picked_s[:], x_scale_rows[:].indirect(offs_list[:]))
+        w1_w = deal_words(w1_raw, "w1_w")
+        picked_w = reused.tile([P, S], U32, name="picked_w", offset=3 * PAGE_BYTES, align_bytes=64)
+        nc.vector.tensor_copy(picked_w[:], x_table[:].bitcast(U32).indirect(offs_list[:]))
+        w1_s = deal_scales(w1_scale_rows, "w1_s")
+        hashed_w = reused.tile([P, S], U32, name="hashed_w", offset=2 * PAGE_BYTES, align_bytes=64)
+        nc.vector.tensor_copy(hashed_w[:], x_table[:].bitcast(U32).indirect(hz_list[:]))
+        w2_w = deal_words(w23_raw, "w2_w")
+        w2_s = deal_scales(w2_scale_rows, "w2_s")
+
+        w3_scale_rows = tile([P, S], U8, "w3_scale_rows", after="w1_raw")
+        nc.gpsimd.memset(w3_scale_rows[:].bitcast(I32), 0)
+        load_scale_rows(w3_scale_rows, w3_scales)
+        nc.sync.dma_start(w23_raw[:], words_view(w3_words))
+        page = [reused.tile([P, U], F32, name=f"page{t}", offset=PAGE_BYTES * t) for t in range(PACK)]
+        mem_rows = mem.rearrange("(p t) w -> t p w", t=PACK)
+        for t in range(PACK):
             nc.sync.dma_start(page[t][:], mem_rows[t])
 
         def product(acc, w_w, w_s, t, a_w, a_s):
             cols = slice(t * P, (t + 1) * P)
-            nc.tensor.matmul_mx(out=acc, lhsT=w_w[:, cols].bitcast(FP8X4), lhsT_scale=w_s[:, cols],
-                                rhs=a_w.bitcast(FP8X4), rhs_scale=a_s, start=True, stop=True)
+            nc.tensor.matmul_mx(
+                out=acc, lhsT=w_w[:, cols].bitcast(FP8X4), lhsT_scale=w_s[:, cols],
+                rhs=a_w.bitcast(FP8X4), rhs_scale=a_s, start=True, stop=True,
+            )
 
         d_ps = [psum.tile([P, S], F32, name=f"d_ps{t}") for t in range(PACK)]
         d_sb = [tile([P, S], F32, f"d_sb{t}") for t in range(PACK)]
-        y_sb = [tile([P, S], F32, f"y_sb{t}") for t in range(PACK)]
+        y_sb = [tile([P, S], F32, f"y_sb{t}") for t in range(2)]
+        y_sb += [
+            reused.tile([P, S], F32, name=f"y_sb{2 + e}", offset=PACK * PAGE_BYTES + ROW_BYTES * e, align_bytes=64)
+            for e in range(2)
+        ]
         y_ps = [psum.tile([P, S], F32, name=f"y_ps{t}", tag=f"bank{t}") for t in range(PACK)]
-        for t in range(PACK):
-            product(d_ps[t][:], w2_w, w2_s, t, xh_w[:], xh_s[:])
-        for t in range(PACK):
-            product(y_ps[t][:], w1_w, w1_s, t, xq_w[:], xq_s[:])
+        for pair in range(2):
+            for t in (2 * pair, 2 * pair + 1):
+                product(y_ps[t][:], w1_w, w1_s, t, picked_w[:], picked_s[:])
+            for t in (2 * pair, 2 * pair + 1):
+                product(d_ps[t][:], w2_w, w2_s, t, hashed_w[:], hashed_s[:])
 
         pulled = tile([P, PACK, S], F32, "pulled")
         held = tile([P, PACK, S], F32, "held")
         gate = [tile([P, S], F32, f"gate{t}") for t in range(PACK)]
         diff = [tile([P, S], F32, f"diff{t}") for t in range(PACK)]
+        far = [tile([P, S], F32, f"far{t}") for t in range(PACK)]
+        near = {t: tile([P, S], F32, f"near{t}") for t in (0, LAST)}
+        halves = (slice(0, HALF), slice(HALF, S))
 
-        def front(t):
-            nc.scalar.copy(d_sb[t][:], d_ps[t][:])
-            far = tile([P, S], F32, f"far{t}")
-            for c0 in (0, HALF):
-                nc.scalar.activation(far[:, c0 : c0 + HALF], d_sb[t][:].indirect(entries(n2_sb, c0, HALF)), ACT.Copy)
-            if t < 2:
-                nc.vector.tensor_scalar(y_sb[t][:], y_ps[t][:], gain[:, t : t + 1], None, ALU.mult)
-            nc.vector.tensor_tensor(diff[t][:], far[:], d_ps[t][:], ALU.subtract)
+        def fetch_on_scalar(dst, window, lst):
+            for cols in halves:
+                nc.scalar.activation(dst[:, cols], window[:].indirect(entries(lst, cols.start, HALF)), ACT.Copy)
 
-        def back(t):
+        def subtract_d(t):
+            nc.vector.tensor_tensor(diff[t][:], far[t][:], d_ps[t][:], ALU.subtract)
+
+        def blend(t):
             nc.scalar.activation(gate[t][:], diff[t][:], ACT.Sigmoid)
-            if t in (1, 2):
-                nc.scalar.activation(y_sb[t + 1][:], y_ps[t + 1][:], ACT.Copy, scale=gain[:, t + 1 : t + 2])
-            if t < PACK - 1:
-                for c0 in (0, HALF):
-                    nc.vector.tensor_tensor(pulled[:, t, c0 : c0 + HALF], y_sb[t][:].indirect(entries(n1_sb, c0, HALF)), gate[t][:, c0 : c0 + HALF], ALU.mult)
+            if t not in near:
+                for cols in halves:
+                    looked_up = y_sb[t][:].indirect(entries(n1_list, cols.start, HALF))
+                    nc.vector.tensor_tensor(pulled[:, t, cols], looked_up, gate[t][:, cols], ALU.mult)
             nc.vector.scalar_tensor_tensor(held[:, t, :], gate[t][:], 1.0, y_sb[t][:], ALU.subtract, ALU.mult)
-            if t == PACK - 1:
-                near = tile([P, S], F32, "near")
-                for c0 in (0, HALF):
-                    nc.scalar.activation(near[:, c0 : c0 + HALF], y_sb[t][:].indirect(entries(n1_sb, c0, HALF)), ACT.Copy)
-                nc.vector.tensor_tensor(pulled[:, t, :], near[:], gate[t][:], ALU.mult)
+            if t in near:
+                nc.vector.tensor_tensor(pulled[:, t, :], near[t][:], gate[t][:], ALU.mult)
 
-        front(0)
+        for t in (0, 1):
+            nc.scalar.activation(y_sb[t][:], y_ps[t][:], ACT.Copy, scale=gain[:, t : t + 1])
+        fetch_on_scalar(near[0], y_sb[0], n1_list)
+        nc.vector.tensor_copy(d_sb[0][:], d_ps[0][:])
+        nc.vector.tensor_scalar(y_sb[2][:], y_ps[2][:], gain[:, 2:3], None, ALU.mult)
+        for cols in halves:
+            nc.vector.tensor_copy(far[0][:, cols], d_sb[0][:].indirect(entries(n2_list, cols.start, HALF)))
+        nc.vector.tensor_scalar(y_sb[3][:], y_ps[3][:], gain[:, 3:4], None, ALU.mult)
+        subtract_d(0)
+        nc.scalar.copy(d_sb[1][:], d_ps[1][:])
         for t in range(PACK):
+            if t + 2 < PACK:
+                nc.scalar.copy(d_sb[t + 2][:], d_ps[t + 2][:])
             if t + 1 < PACK:
-                front(t + 1)
-            if t == 1:
-                w3_s = deal_scales(w2s_raw, "w3_s")
-            if t == 3:
-                w3_w = deal_words(ww_raw[1], "w3_w")
-            back(t)
+                fetch_on_scalar(far[t + 1], d_sb[t + 1], n2_list)
+                subtract_d(t + 1)
+            else:
+                fetch_on_scalar(near[LAST], y_sb[LAST], n1_list)
+            blend(t)
+        w3_w = deal_words(w23_raw, "w3_w", after=f"diff{LAST}")
 
         z_bf = [tile([P, HALF * PACK], BF16, f"z_bf{half}") for half in range(2)]
         z_w = [tile([P, HALF], U32, f"z_w{half}") for half in range(2)]
         z_s = [tile([P, HALF], U8, f"z_s{half}") for half in range(2)]
         h_sb = tile([P, PACK, S], F32, "h_sb")
-        for half in range(2):
-            cols = slice(half * HALF, (half + 1) * HALF)
+        for half, cols in enumerate(halves):
             nc.vector.tensor_tensor(
-                z_bf[half][:].rearrange("p (c i t) -> p c t i", i=4, t=PACK),
-                pulled[:, :, cols].rearrange("p t (c i) -> p c t i", i=4),
-                held[:, :, cols].rearrange("p t (c i) -> p c t i", i=4),
-                ALU.subtract,
+                woven(z_bf[half][:]), by_lines(pulled[:, :, cols]), by_lines(held[:, :, cols]), ALU.subtract
             )
+            if half == 0:
+                w3_s = deal_scales(w3_scale_rows, "w3_s", after=f"near{LAST}")
             nc.vector.quantize_mx(out=z_w[half][:].bitcast(FP8X4), scales=z_s[half][:], in_=z_bf[half][:])
             for pair in range(2):
                 h_ps = psum.tile([P, 2, HALF], F32, name=f"h_ps{half}_{pair}", tag=f"bank{2 * half + pair}")
@@ -183,56 +221,43 @@ def tile_picked_twhpullbpagem_none_po_kernel(
 
         result = tile([P, PACK, U], F32, "result")
         out_rows = out_0.rearrange("(p t) w -> t p w", t=PACK)
-        CH = 512
-
-        def scatter(t):
+        for t in range(PACK):
             width = HALF if t == 0 else S
             for c0 in range(0, S, width):
-                nc.vector.tensor_copy(page[t][:].indirect(entries(n3_sb, c0, width)), h_sb[:, t, c0 : c0 + width])
+                nc.vector.tensor_copy(page[t][:].indirect(entries(n3_list, c0, width)), h_sb[:, t, c0 : c0 + width])
 
-        def finish(t):
-            for c0 in range(0, U, CH):
-                other = tile([P, CH], F32, f"other{t}_{c0}")
-                nc.scalar.activation(other[:], page[t][:].indirect(entries(n4_sb, c0, CH)), ACT.Copy, scale=-0.5)
-                adder = nc.gpsimd if t < PACK - 1 else nc.vector
-                adder.tensor_tensor(result[:, t, c0 : c0 + CH], other[:], page[t][:, c0 : c0 + CH], ALU.add)
-                nc.sync.dma_start(out_rows[t][:, c0 : c0 + CH], result[:, t, c0 : c0 + CH])
+        for t in range(LAST):
+            for c0 in range(0, U, PAGE_HALF):
+                cols = slice(c0, c0 + PAGE_HALF)
+                other = tile([P, PAGE_HALF], F32, f"other{t}_{c0}")
+                nc.scalar.activation(other[:], page[t][:].indirect(entries(n4_list, c0, PAGE_HALF)), ACT.Copy, scale=-0.5)
+                nc.gpsimd.tensor_tensor(result[:, t, cols], other[:], page[t][:, cols], ALU.add)
+                nc.sync.dma_start(out_rows[t][:, cols], result[:, t, cols])
 
-        for t in range(PACK):
-            scatter(t)
-        for t in range(PACK - 1):
-            finish(t)
-
-        o_w = tile([P, U], U32, "o_w")
-        o_s = tile([P, U], U8, "o_s")
-        QC = 256
+        out_w = tile([P, U], U32, "out_w")
+        out_s = tile([P, U], U8, "out_s")
         out_words = words_view(out_1)
-        last = PACK - 1
-        order = (3, 0, 1, 2)
-        for k in order:
-            c0 = k * QC
-            other = tile([P, QC], F32, f"other{last}_{c0}")
-            looked = page[last][:].indirect(entries(n4_sb, c0, QC))
-            if k == 3:
-                nc.vector.tensor_copy(other[:], looked)
+        chunks = [slice(c0, c0 + CHUNK) for c0 in range(0, U, CHUNK)]
+        arrival = chunks[-1:] + chunks[:-1]
+        for cols in arrival:
+            other = tile([P, CHUNK], F32, f"other{LAST}_{cols.start}")
+            looked_up = page[LAST][:].indirect(entries(n4_list, cols.start, CHUNK))
+            if cols == chunks[-1]:
+                nc.vector.tensor_copy(other[:], looked_up)
             else:
-                nc.scalar.activation(other[:], looked, ACT.Copy)
-            nc.vector.scalar_tensor_tensor(result[:, last, c0 : c0 + QC], other[:], -0.5, page[last][:, c0 : c0 + QC], ALU.mult, ALU.add)
-        for c0 in (CH, 0):
-            nc.sync.dma_start(out_rows[last][:, c0 : c0 + CH], result[:, last, c0 : c0 + CH])
-        o_bf = {}
-        for n, k in enumerate(order):
-            c0 = k * QC
-            o_bf[k] = tile([P, QC * PACK], BF16, f"o_bf{k}")
-            dst = o_bf[k][:].rearrange("p (c i t) -> p c t i", i=4, t=PACK)
-            src = result[:, :, c0 : c0 + QC].rearrange("p t (c i) -> p c t i", i=4)
-            if n % 2 == 0:
-                nc.vector.tensor_copy(dst, src)
-            else:
-                nc.scalar.copy(dst, src)
-        for k in (3, 1, 0, 2):
-            c0 = k * QC
-            nc.vector.quantize_mx(out=o_w[:, c0 : c0 + QC].bitcast(FP8X4), scales=o_s[:, c0 : c0 + QC], in_=o_bf[k][:])
-            nc.sync.dma_start(out_words[:, c0 : c0 + QC], o_w[:, c0 : c0 + QC].bitcast(I32))
-        for q in range(4):
-            nc.sync.dma_start(out_2[0, 4 * q : 4 * q + 4, :].bitcast(I32), o_s[32 * q : 32 * q + 4, :].bitcast(I32))
+                nc.scalar.activation(other[:], looked_up, ACT.Copy)
+            nc.vector.scalar_tensor_tensor(result[:, LAST, cols], other[:], -0.5, page[LAST][:, cols], ALU.mult, ALU.add)
+        for c0 in (PAGE_HALF, 0):
+            nc.sync.dma_start(out_rows[LAST][:, c0 : c0 + PAGE_HALF], result[:, LAST, c0 : c0 + PAGE_HALF])
+        out_bf = {}
+        for n, cols in enumerate(arrival):
+            out_bf[cols.start] = tile([P, CHUNK * PACK], BF16, f"out_bf{cols.start}")
+            weave = nc.vector.tensor_copy if n % 2 == 0 else nc.scalar.copy
+            weave(woven(out_bf[cols.start][:]), by_lines(result[:, :, cols]))
+        for cols in arrival[0::2] + arrival[1::2]:
+            nc.vector.quantize_mx(out=out_w[:, cols].bitcast(FP8X4), scales=out_s[:, cols], in_=out_bf[cols.start][:])
+            nc.sync.dma_start(out_words[:, cols], out_w[:, cols].bitcast(I32))
+        for q in range(P // QUADRANT):
+            nc.sync.dma_start(
+                out_2[0, 4 * q : 4 * q + 4, :].bitcast(I32), out_s[QUADRANT * q : QUADRANT * q + 4, :].bitcast(I32)
+            )

@@ -85,6 +85,9 @@ def tile_picked_twhpullbpagem_none_po_kernel(
         )
         nc.gpsimd.memset(w1_scale_rows[:].bitcast(I32), 0)
         nc.gpsimd.memset(w2_scale_rows[:].bitcast(I32), 0)
+        warm = tile([P, 8], F32, "warm")
+        nc.vector.memset(warm[:, 0:1], 0.0)
+        nc.scalar.activation(warm[:, 4:5], warm[:, 0:1], ACT.Sigmoid)
         gain = tile([P, PACK], F32, "gain")
         nc.gpsimd.dma_start(gain[:], gn.rearrange("(p t) o -> p (t o)", t=PACK))
         hz_list = load_list(hz, "hz_list")

@@ -261,6 +261,7 @@ def tile_picked_twhpullbpagem_none_po_kernel(
             nc.vector.quantize_mx(out=out_w[:, cols].bitcast(FP8X4), scales=out_s[:, cols], in_=out_bf[cols.start][:])
             nc.sync.dma_start(out_words[:, cols], out_w[:, cols].bitcast(I32))
         for q in range(P // QUADRANT):
-            nc.sync.dma_start(
+            queue = nc.scalar if q % 2 == 0 else nc.sync
+            queue.dma_start(
                 out_2[0, 4 * q : 4 * q + 4, :].bitcast(I32), out_s[QUADRANT * q : QUADRANT * q + 4, :].bitcast(I32)
             )

from contextlib import ExitStack

import concourse.mybir as mybir

F32 = mybir.dt.float32
BF16 = mybir.dt.bfloat16
I32 = mybir.dt.int32
U32 = mybir.dt.uint32
U16 = mybir.dt.uint16
U8 = mybir.dt.uint8
FP8X4 = mybir.dt.float8_e4m3fn_x4
ACT = mybir.ActivationFunctionType
ALU = mybir.AluOpType

P = 128
PACK = 4
LAST = PACK - 1
QUADRANT = 32
GROUP = 16
T, S, U = 2048, 512, 1024
HALF = S // 2
PAGE_HALF = U // 2
CHUNK = U // 4
LINE = 4
PAGE_BYTES = 4 * U
ROW_BYTES = 4 * S
FLOPS = 3 * 2 * 512 * 512 * 512


def tile_picked_twhpullbpagem_none_po_kernel(
    tc, x_words, x_scales, w1_words, w1_scales, w2_words, w2_scales, gn, w3_words, w3_scales,
    mem, offs, hz, n1, n2, n3, n4, out_0, out_1, out_2,
):
    nc = tc.nc
    with ExitStack() as ctx:
        keep = ctx.enter_context(tc.tile_pool(name="keep", bufs=1))
        reused = ctx.enter_context(tc.tile_pool(name="reused", bufs=1))
        psum = ctx.enter_context(tc.psum_pool(name="psum", bufs=1))

        def tile(shape, dtype, name, after=""):
            return keep.tile(shape, dtype, name=name, tag=after or name, align_bytes=64)

        def load_list(src, name):
            dst = tile(list(src.shape), U16, name)
            nc.sync.dma_start(dst[:], src)
            return dst

        def words_view(src):
            return src[0].rearrange("p n t -> p (n t)").bitcast(I32)

        def entries(lst, start, count):
            return lst[:, start // GROUP : (start + count) // GROUP]

        def load_scale_rows(dst, src):
            for q in range(P // QUADRANT):
                nc.sync.dma_start(
                    dst[QUADRANT * q : QUADRANT * q + 4, :].bitcast(I32), src[0, 4 * q : 4 * q + 4, :].bitcast(I32)
                )

        def deal_words(raw, name, after=""):
            dealt = tile([P, S], U32, name, after)
            nc.scalar.copy(
                dealt[:].rearrange("p (t m) -> p m t", t=PACK), raw[:].bitcast(U32).rearrange("p (m t) -> p m t", t=PACK)
            )
            return dealt

        def deal_scales(raw, name, after=""):
            dealt = tile([P, S], U8, name, after)
            nc.vector.tensor_copy(
                dealt[:].rearrange("p (t m) -> p m t", t=PACK), raw[:].rearrange("p (m t) -> p m t", t=PACK)
            )
            return dealt

        def woven(dst):
            return dst.rearrange("p (c i t) -> p c t i", i=LINE, t=PACK)

        def by_lines(src):
            return src.rearrange("p t (c i) -> p c t i", i=LINE)

        x_scale_rows = tile([P, T], U8, "x_scale_rows")
        nc.gpsimd.memset(x_scale_rows[:].bitcast(I32), 0)
        w1_scale_rows = reused.tile([P, S], U8, name="w1_scale_rows", offset=2 * PAGE_BYTES, align_bytes=64)
        w2_scale_rows = reused.tile(
            [P, S], U8, name="w2_scale_rows", offset=PACK * PAGE_BYTES + ROW_BYTES - S // 2, align_bytes=64
        )
        nc.gpsimd.memset(w1_scale_rows[:].bitcast(I32), 0)
        nc.gpsimd.memset(w2_scale_rows[:].bitcast(I32), 0)
        warm = tile([P, 8], F32, "warm")
        nc.vector.memset(warm[:, 0:1], 0.0)
        nc.scalar.activation(warm[:, 4:5], warm[:, 0:1], ACT.Sigmoid)
        gain = tile([P, PACK], F32, "gain")
        nc.gpsimd.dma_start(gain[:], gn.rearrange("(p t) o -> p (t o)", t=PACK))
        hz_list = load_list(hz, "hz_list")
        offs_list = load_list(offs, "offs_list")
        rows_dst, rows_src = x_scale_rows[:].bitcast(I32), x_scales[0].bitcast(I32)
        for e in range(2):
            nc.sync.dma_start(rows_dst[e:P:GROUP, :], rows_src[e:16:2, :])
        for r in (2, 3):
            nc.sync.dma_start(rows_dst[r:P:QUADRANT, :], rows_src[r:16:4, :])
        x_table = reused.tile([P, T], I32, name="x_table", offset=0)
        nc.sync.dma_start(x_table[:], words_view(x_words))
        w1_raw = tile([P, S], I32, "w1_raw")
        w23_raw = tile([P, S], I32, "w23_raw")
        nc.sync.dma_start(w1_raw[:], words_view(w1_words))
        load_scale_rows(w1_scale_rows, w1_scales)
        nc.sync.dma_start(w23_raw[:], words_view(w2_words))
        n1_list = load_list(n1, "n1_list")

        hashed_rows = tile([P, S], U8, "hashed_rows")
        nc.vector.tensor_copy(hashed_rows[:], x_scale_rows[:].indirect(hz_list[:]))
        hashed_s = tile([P, S], U8, "hashed_s")
        nc.vector.tensor_copy(hashed_s[:].bitcast(I32), hashed_rows[:].bitcast(I32))
        for e in range(2):
            nc.sync.dma_start(
                hashed_s[:].bitcast(I32)[2 + e : P : QUADRANT, :], hashed_rows[:].bitcast(I32)[GROUP + e : P : QUADRANT, :]
            )
        load_scale_rows(w2_scale_rows, w2_scales)
        n2_list = load_list(n2, "n2_list")
        n3_list = load_list(n3, "n3_list")
        n4_list = load_list(n4, "n4_list")
        picked_s = tile([P, S], U8, "picked_s")
        nc.vector.tensor_copy(picked_s[:], x_scale_rows[:].indirect(offs_list[:]))
        w1_w = deal_words(w1_raw, "w1_w")
        picked_w = reused.tile([P, S], U32, name="picked_w", offset=3 * PAGE_BYTES, align_bytes=64)
        nc.vector.tensor_copy(picked_w[:], x_table[:].bitcast(U32).indirect(offs_list[:]))
        w1_s = deal_scales(w1_scale_rows, "w1_s")
        hashed_w = reused.tile([P, S], U32, name="hashed_w", offset=2 * PAGE_BYTES, align_bytes=64)
        nc.vector.tensor_copy(hashed_w[:], x_table[:].bitcast(U32).indirect(hz_list[:]))
        w2_w = deal_words(w23_raw, "w2_w")
        w2_s = deal_scales(w2_scale_rows, "w2_s")

        w3_scale_rows = tile([P, S], U8, "w3_scale_rows", after="w1_raw")
        nc.gpsimd.memset(w3_scale_rows[:].bitcast(I32), 0)
        load_scale_rows(w3_scale_rows, w3_scales)
        nc.sync.dma_start(w23_raw[:], words_view(w3_words))
        page = [reused.tile([P, U], F32, name=f"page{t}", offset=PAGE_BYTES * t) for t in range(PACK)]
        mem_rows = mem.rearrange("(p t) w -> t p w", t=PACK)
        for t in range(PACK):
            nc.sync.dma_start(page[t][:], mem_rows[t])

        def product(acc, w_w, w_s, t, a_w, a_s):
            cols = slice(t * P, (t + 1) * P)
            nc.tensor.matmul_mx(
                out=acc, lhsT=w_w[:, cols].bitcast(FP8X4), lhsT_scale=w_s[:, cols],
                rhs=a_w.bitcast(FP8X4), rhs_scale=a_s, start=True, stop=True,
            )

        d_ps = [psum.tile([P, S], F32, name=f"d_ps{t}") for t in range(PACK)]
        d_sb = [tile([P, S], F32, f"d_sb{t}") for t in range(PACK)]
        y_sb = [tile([P, S], F32, f"y_sb{t}") for t in range(2)]
        y_sb += [
            reused.tile([P, S], F32, name=f"y_sb{2 + e}", offset=PACK * PAGE_BYTES + ROW_BYTES * e, align_bytes=64)
            for e in range(2)
        ]
        y_ps = [psum.tile([P, S], F32, name=f"y_ps{t}", tag=f"bank{t}") for t in range(PACK)]
        for pair in range(2):
            for t in (2 * pair, 2 * pair + 1):
                product(y_ps[t][:], w1_w, w1_s, t, picked_w[:], picked_s[:])
            for t in (2 * pair, 2 * pair + 1):
                product(d_ps[t][:], w2_w, w2_s, t, hashed_w[:], hashed_s[:])

        pulled = tile([P, PACK, S], F32, "pulled")
        held = tile([P, PACK, S], F32, "held")
        gate = [tile([P, S], F32, f"gate{t}") for t in range(PACK)]
        diff = [tile([P, S], F32, f"diff{t}") for t in range(PACK)]
        far = [tile([P, S], F32, f"far{t}") for t in range(PACK)]
        near = {t: tile([P, S], F32, f"near{t}") for t in (0, LAST)}
        halves = (slice(0, HALF), slice(HALF, S))

        def fetch_on_scalar(dst, window, lst):
            for cols in halves:
                nc.scalar.activation(dst[:, cols], window[:].indirect(entries(lst, cols.start, HALF)), ACT.Copy)

        def subtract_d(t):
            nc.vector.tensor_tensor(diff[t][:], far[t][:], d_ps[t][:], ALU.subtract)

        def blend(t):
            nc.scalar.activation(gate[t][:], diff[t][:], ACT.Sigmoid)
            if t not in near:
                for cols in halves:
                    looked_up = y_sb[t][:].indirect(entries(n1_list, cols.start, HALF))
                    nc.vector.tensor_tensor(pulled[:, t, cols], looked_up, gate[t][:, cols], ALU.mult)
            nc.vector.scalar_tensor_tensor(held[:, t, :], gate[t][:], 1.0, y_sb[t][:], ALU.subtract, ALU.mult)
            if t in near:
                nc.vector.tensor_tensor(pulled[:, t, :], near[t][:], gate[t][:], ALU.mult)

        for t in (0, 1):
            nc.scalar.activation(y_sb[t][:], y_ps[t][:], ACT.Copy, scale=gain[:, t : t + 1])
        fetch_on_scalar(near[0], y_sb[0], n1_list)
        nc.vector.tensor_copy(d_sb[0][:], d_ps[0][:])
        nc.vector.tensor_scalar(y_sb[2][:], y_ps[2][:], gain[:, 2:3], None, ALU.mult)
        for cols in halves:
            nc.vector.tensor_copy(far[0][:, cols], d_sb[0][:].indirect(entries(n2_list, cols.start, HALF)))
        nc.vector.tensor_scalar(y_sb[3][:], y_ps[3][:], gain[:, 3:4], None, ALU.mult)
        subtract_d(0)
        nc.scalar.copy(d_sb[1][:], d_ps[1][:])
        for t in range(PACK):
            if t + 2 < PACK:
                nc.scalar.copy(d_sb[t + 2][:], d_ps[t + 2][:])
            if t + 1 < PACK:
                fetch_on_scalar(far[t + 1], d_sb[t + 1], n2_list)
                subtract_d(t + 1)
            else:
                fetch_on_scalar(near[LAST], y_sb[LAST], n1_list)
            blend(t)
        w3_w = deal_words(w23_raw, "w3_w", after=f"diff{LAST}")

        z_bf = [tile([P, HALF * PACK], BF16, f"z_bf{half}") for half in range(2)]
        z_w = [tile([P, HALF], U32, f"z_w{half}") for half in range(2)]
        z_s = [tile([P, HALF], U8, f"z_s{half}") for half in range(2)]
        h_sb = tile([P, PACK, S], F32, "h_sb")
        for half, cols in enumerate(halves):
            nc.vector.tensor_tensor(
                woven(z_bf[half][:]), by_lines(pulled[:, :, cols]), by_lines(held[:, :, cols]), ALU.subtract
            )
            if half == 0:
                w3_s = deal_scales(w3_scale_rows, "w3_s", after=f"near{LAST}")
            nc.vector.quantize_mx(out=z_w[half][:].bitcast(FP8X4), scales=z_s[half][:], in_=z_bf[half][:])
            for pair in range(2):
                h_ps = psum.tile([P, 2, HALF], F32, name=f"h_ps{half}_{pair}", tag=f"bank{2 * half + pair}")
                for e in range(2):
                    product(h_ps[:, e, :], w3_w, w3_s, 2 * pair + e, z_w[half][:], z_s[half][:])
                nc.scalar.copy(h_sb[:, 2 * pair : 2 * pair + 2, cols], h_ps[:])

        result = tile([P, PACK, U], F32, "result")
        out_rows = out_0.rearrange("(p t) w -> t p w", t=PACK)
        for t in range(PACK):
            width = HALF if t == 0 else S
            for c0 in range(0, S, width):
                nc.vector.tensor_copy(page[t][:].indirect(entries(n3_list, c0, width)), h_sb[:, t, c0 : c0 + width])

        for t in range(LAST):
            for c0 in range(0, U, PAGE_HALF):
                cols = slice(c0, c0 + PAGE_HALF)
                other = tile([P, PAGE_HALF], F32, f"other{t}_{c0}")
                nc.scalar.activation(other[:], page[t][:].indirect(entries(n4_list, c0, PAGE_HALF)), ACT.Copy, scale=-0.5)
                nc.gpsimd.tensor_tensor(result[:, t, cols], other[:], page[t][:, cols], ALU.add)
                nc.sync.dma_start(out_rows[t][:, cols], result[:, t, cols])

        out_w = tile([P, U], U32, "out_w")
        out_s = tile([P, U], U8, "out_s")
        out_words = words_view(out_1)
        chunks = [slice(c0, c0 + CHUNK) for c0 in range(0, U, CHUNK)]
        arrival = chunks[-1:] + chunks[:-1]
        for cols in arrival:
            other = tile([P, CHUNK], F32, f"other{LAST}_{cols.start}")
            looked_up = page[LAST][:].indirect(entries(n4_list, cols.start, CHUNK))
            if cols == chunks[-1]:
                nc.vector.tensor_copy(other[:], looked_up)
            else:
                nc.scalar.activation(other[:], looked_up, ACT.Copy)
            nc.vector.scalar_tensor_tensor(result[:, LAST, cols], other[:], -0.5, page[LAST][:, cols], ALU.mult, ALU.add)
        for c0 in (PAGE_HALF, 0):
            nc.sync.dma_start(out_rows[LAST][:, c0 : c0 + PAGE_HALF], result[:, LAST, c0 : c0 + PAGE_HALF])
        out_bf = {}
        for n, cols in enumerate(arrival):
            out_bf[cols.start] = tile([P, CHUNK * PACK], BF16, f"out_bf{cols.start}")
            weave = nc.vector.tensor_copy if n % 2 == 0 else nc.scalar.copy
            weave(woven(out_bf[cols.start][:]), by_lines(result[:, :, cols]))
        for cols in arrival[0::2] + arrival[1::2]:
            nc.vector.quantize_mx(out=out_w[:, cols].bitcast(FP8X4), scales=out_s[:, cols], in_=out_bf[cols.start][:])
            nc.sync.dma_start(out_words[:, cols], out_w[:, cols].bitcast(I32))
        for q in range(P // QUADRANT):
            queue = nc.scalar if q % 2 == 0 else nc.sync
            queue.dma_start(
                out_2[0, 4 * q : 4 * q + 4, :].bitcast(I32), out_s[QUADRANT * q : QUADRANT * q + 4, :].bitcast(I32)
            )
